import numpy as np
import ml_dtypes


def mxq(x, axis, fmt="e4m3"):
    dtype, down = {"e4m3": (ml_dtypes.float8_e4m3fn, 7), "e5m2": (ml_dtypes.float8_e5m2, 14)}[fmt]
    v = np.moveaxis(np.asarray(x, np.float32).astype(ml_dtypes.bfloat16).astype(np.float64), axis, -1)
    blocks = v.reshape(v.shape[:-1] + (-1, 32))
    amax = np.abs(blocks).max(-1, keepdims=True)
    byte = np.maximum(np.where(amax > 0, np.frexp(amax)[1] - 1 + 127, 0) - down, 1)
    scale = np.exp2(byte - 127.0)
    codes = (blocks / scale).astype(np.float32).astype(dtype).astype(np.float64)
    return np.moveaxis((codes * scale).reshape(v.shape), -1, axis)


WIDE = False


def mx_kscale(k):
    if not WIDE:
        return np.ones(k)
    levels = np.array([10, -10, 5, -5, 0])
    if k % 512:
        return np.exp2(np.random.permutation(np.resize(levels, k // 32))).repeat(32)
    a = np.empty((k // 512, 16))
    for p in range(k // 512):
        a[p, :8] = np.random.permutation(np.resize(levels, 8))
        for g in range(8):
            far = levels[np.abs(levels - a[p, g]) >= 10]
            a[p, g + 8] = far[np.random.randint(len(far))]
    return np.exp2(a.ravel()).repeat(32)


BF16 = ml_dtypes.bfloat16


def bf(x):
    return np.asarray(x, np.float32).astype(BF16)


def f64(x):
    return np.asarray(x).astype(np.float64)


E2M1 = np.array([0.0, 0.5, 1.0, 1.5, 2.0, 3.0, 4.0, 6.0, -0.0, -0.5, -1.0, -1.5, -2.0, -3.0, -4.0, -6.0])


def pack_weight(w, fmt):
    k, n = w.shape
    w = f64(bf(w)).reshape(k // 32, 32, n)
    amax = np.abs(w).max(1)
    if fmt == "e4m3":
        byte = np.frexp(amax)[1] - 1 + 127 - 7
    else:
        mant, ex = np.frexp(amax / 6.0)
        byte = np.where(mant > 0.5, ex, ex - 1) + 127
    byte = np.clip(np.where(amax > 0, byte, 1), 1, 254)
    scaled = (w * np.exp2(127.0 - byte)[:, None, :]).reshape(k, n).astype(np.float32)
    by_word = np.ascontiguousarray(scaled.reshape(k // 512, 128, 4, n).transpose(0, 1, 3, 2))
    if fmt == "e4m3":
        words = by_word.astype(ml_dtypes.float8_e4m3fn).view(np.uint8)
    else:
        c = by_word.astype(ml_dtypes.float4_e2m1fn).view(np.uint8) & 0xF
        words = c[..., 0::2] | (c[..., 1::2] << 4)
    return np.ascontiguousarray(words), np.ascontiguousarray(byte.astype(np.uint8).reshape(k // 512, 16, n))


def unpack_weight(words, scales, fmt):
    g, p, n, _ = words.shape
    if fmt == "e4m3":
        vals = np.ascontiguousarray(words).view(ml_dtypes.float8_e4m3fn).astype(np.float64)
    else:
        nib = np.empty((g, p, n, 4), np.uint8)
        nib[..., 0::2] = words & 0xF
        nib[..., 1::2] = words >> 4
        vals = E2M1[nib]
    vals = vals * np.repeat(np.exp2(scales.astype(np.float64) - 127.0), 8, axis=1)[..., None]
    return vals.transpose(0, 1, 3, 2).reshape(g * 512, n)
def pack4(w):
    words, scales = pack_weight(w, "e2m1")
    return words.reshape(words.shape[0], 128, -1), scales


def unpack4(words, scales):
    return unpack_weight(words.reshape(words.shape[0], 128, -1, 2), scales, "e2m1")


def planes(Y):
    n, m = Y.shape
    b = f64(bf(Y)).reshape(n // 32, 32, m)
    amax = np.abs(b).max(1)
    byte = np.clip(np.where(amax > 0, np.frexp(amax)[1] - 1 + 127 - 7, 1), 1, 254)
    codes = (b * np.exp2(127.0 - byte)[:, None, :]).reshape(n, m).astype(np.float32).astype(ml_dtypes.float8_e4m3fn).view(np.uint8)
    words = codes.reshape(n // 512, 128, 4, m).transpose(0, 1, 3, 2)
    return np.ascontiguousarray(words), np.ascontiguousarray(byte.astype(np.uint8).reshape(n // 512, 16, m))


SURFERS, PAGES = 1024, 2048


def setup_inputs():
    s = mx_kscale(PAGES)
    ranks = np.exp(0.8 * np.random.randn(SURFERS, PAGES) - 0.64)
    pull = np.exp(0.8 * np.random.randn(PAGES))
    links = np.random.randn(PAGES, PAGES) / np.sqrt(PAGES) * pull[None, :]
    links_words, links_scales = pack4(links / s[:, None])
    damp = 0.6 + 0.3 * np.random.rand(SURFERS)
    teleport = np.exp(0.5 * np.random.randn(PAGES))
    return {
        "ranks": bf(ranks * s[None, :]),
        "links_words": links_words,
        "links_scales": links_scales,
        "damp": bf(damp),
        "teleport": bf(teleport),
    }

def reference(ranks, links_words, links_scales, damp, teleport):
    d = f64(damp)[:, None]
    flow = mxq(f64(ranks), 1, "e4m3") @ unpack4(links_words, links_scales)
    y = d * flow + (1.0 - d) * f64(teleport)[None, :]
    Y = y.T
    words, scales = planes(Y)
    return y, words, scales

@@ -1,0 +1,255 @@
+from contextlib import ExitStack
+
+import concourse.mybir as mybir
+from concourse.masks import make_identity
+
+SURFERS, PAGES = 1024, 2048
+FLOPS = 2 * SURFERS * PAGES * PAGES
+
+F32 = mybir.dt.float32
+BF16 = mybir.dt.bfloat16
+I32 = mybir.dt.int32
+U32 = mybir.dt.uint32
+U8 = mybir.dt.uint8
+FP8X4 = mybir.dt.float8_e4m3fn_x4
+FP4X4 = mybir.dt.float4_e2m1fn_x4
+ALU = mybir.AluOpType
+ACT = mybir.ActivationFunctionType
+
+P = 128
+GROUP = 512
+GROUPS = PAGES // GROUP
+TILES = SURFERS // P
+UNITS = GROUPS * TILES
+QUADRANTS = 4
+SCALE_ROWS = 4
+
+RANK_TURNS = {0: [0, 1], 1: [2], 2: [3, 4], 4: [5, 6], 6: [7]}
+PAIR_TURNS = {6: [0, 1], 14: [2, 3, 4, 5], 22: [6, 7, 8, 9], 30: [10, 11, 12, 13]}
+QUAD_QUANTS = {7: [0], 14: [1], 15: [2], 22: [3], 23: [4], 30: [5, 6]}
+
+
+def tile_signed_link_rank_step_g4_kernel(
+    tc, ranks, links_words, links_scales, damp, teleport, out_0, out_1, out_2
+):
+    nc = tc.nc
+    with ExitStack() as ctx:
+        keep = ctx.enter_context(tc.tile_pool(name="keep", bufs=1))
+        psum = ctx.enter_context(tc.psum_pool(name="psum", bufs=1))
+        ctx.enter_context(tc.manual_schedule())
+
+        turn_count = []
+
+        def turn_bank():
+            turn_count.append(0)
+            return psum.tile([P, 4, P], F32, name="turn%d" % (len(turn_count) % 4))
+
+        ident = keep.tile([P, P], F32, name="ident")
+        tele_words = keep.tile([P, 8], F32, name="tele_words")
+        damp_rows = keep.tile([TILES, P], BF16, name="damp_rows")
+        damp_wide = keep.tile([P, P], F32, name="damp_wide")
+        damp_col = keep.tile([P, TILES], F32, name="damp_col")
+        rest_col = keep.tile([P, TILES], F32, name="rest_col")
+        tele_all = keep.tile([P, PAGES], BF16, name="tele_all")
+        warm = keep.tile([P, 8], F32, name="warm")
+        raw = [keep.tile([P, PAGES], BF16, name="raw%d" % t) for t in range(TILES)]
+        rank_codes = [keep.tile([P, GROUP], U32, name="rank_codes%d" % t, align_bytes=256) for t in range(TILES)]
+        rank_scales = [keep.tile([P, GROUP], U8, name="rank_scales%d" % t, align_bytes=256) for t in range(TILES)]
+        link_words = [keep.tile([P, GROUPS, 2 * GROUP], U8, name="link_words%d" % n, align_bytes=256) for n in range(GROUPS)]
+        first_scales = keep.tile([P, GROUPS, GROUP], U8, name="first_scales", align_bytes=256)
+        later_scales = keep.tile([P, GROUPS, PAGES - GROUP], U8, name="later_scales", align_bytes=256)
+        out_codes = [keep.tile([P, SURFERS], U32, name="out_codes%d" % n, align_bytes=256) for n in range(GROUPS)]
+        out_scales = keep.tile([P, GROUPS, SURFERS], U8, name="out_scales", align_bytes=256)
+
+        nc.scalar.dma_start(out=tele_words[:], in_=teleport.rearrange("(p c) -> p c", p=P).bitcast(F32))
+        nc.scalar.dma_start(out=damp_rows[:], in_=damp.rearrange("(t p) -> t p", p=P))
+        nc.vector.memset(first_scales[:].rearrange("p g n -> p (g n)").bitcast(I32), 0)
+        nc.vector.memset(warm[:], 0.0)
+        nc.vector.memset(damp_wide[:], 0.0)
+        nc.vector.memset(later_scales[:].rearrange("p g n -> p (g n)").bitcast(I32), 0)
+        nc.scalar.activation(out=warm[:, 4:5], in_=warm[:, 0:1], func=ACT.Copy)
+        make_identity(nc, ident[:])
+
+        def load_ranks(t, c0, c1):
+            nc.sync.dma_start(out=raw[t][:, c0:c1], in_=ranks[P * t : P * (t + 1), c0:c1])
+
+        def load_scales(plane, c0, c1):
+            rows = links_scales[:, :, c0:c1].bitcast(I32).rearrange("g (q r) n -> r q g n", r=SCALE_ROWS)
+            for r in range(SCALE_ROWS):
+                nc.sync.dma_start(out=plane[:].bitcast(I32)[r:P:32, :, :], in_=rows[r])
+
+        def load_links(n, g0, g1):
+            src = links_words[g0:g1, :, 2 * GROUP * n : 2 * GROUP * (n + 1)].bitcast(I32)
+            nc.sync.dma_start(out=link_words[n][:].bitcast(I32)[:, g0:g1, :], in_=src.rearrange("g p w -> p g w"))
+
+        load_ranks(0, 0, PAGES // 2)
+        load_ranks(0, PAGES // 2, PAGES)
+        load_ranks(1, 0, PAGES)
+        load_scales(first_scales, 0, GROUP)
+        load_links(0, 0, 2)
+        load_links(0, 2, 4)
+        for t in range(2, TILES):
+            load_ranks(t, 0, PAGES)
+        load_scales(later_scales, GROUP, PAGES)
+        for n in range(1, GROUPS):
+            load_links(n, 0, GROUPS)
+
+        tele_view = tele_all[:].bitcast(F32).rearrange("p (j h c) -> p h j c", h=2, c=4)
+        for h in range(2):
+            bank = turn_bank()
+            for c in range(4):
+                col = 4 * h + c
+                nc.tensor.transpose(bank[:, c, :], tele_words[:, col : col + 1].to_broadcast([P, P]), ident[:])
+            if h == 0:
+                nc.scalar.copy(out=tele_view[:, h], in_=bank[:].rearrange("p c j -> p j c"))
+            else:
+                nc.vector.tensor_copy(out=tele_view[:, h], in_=bank[:].rearrange("p c j -> p j c"))
+        nc.vector.tensor_copy(out=damp_wide[0:TILES, :], in_=damp_rows[:])
+        bank = turn_bank()
+        nc.tensor.transpose(bank[:, 0, :], damp_wide[:], ident[:])
+        nc.vector.tensor_copy(out=damp_col[:], in_=bank[:, 0, 0:TILES])
+        nc.vector.tensor_scalar(
+            out=rest_col[:], in0=bank[:, 0, 0:TILES], scalar1=-1.0, scalar2=1.0, op0=ALU.mult, op1=ALU.add
+        )
+
+        rank_grouped = {}
+        y_grouped = {}
+        acc = {}
+        jump = {}
+        y = {}
+        y_bf = {}
+
+        def turn_ranks(t):
+            grouped = keep.tile([P, PAGES], BF16, name="rank_grouped%d" % (t % 3), align_bytes=256)
+            rank_grouped[t] = grouped
+            words = raw[t][:].bitcast(F32)
+            for half in range(2):
+                bank = turn_bank()
+                for k in range(4):
+                    g, u = 2 * half + k // 2, k % 2
+                    nc.tensor.transpose(bank[:, k, :], words[:, 256 * g + u : 256 * (g + 1) : 2], ident[:])
+                dst = grouped[:].bitcast(F32)[:, 512 * half : 512 * (half + 1)].rearrange("p (g r u) -> p g r u", g=2, u=2)
+                src = bank[:].rearrange("p (g u) r -> p g r u", u=2)
+                if t == 0 and half == 1:
+                    nc.vector.tensor_copy(out=dst, in_=src)
+                else:
+                    nc.scalar.copy(out=dst, in_=src)
+
+        def quantize_ranks(t):
+            nc.vector.quantize_mx(out=rank_codes[t][:].bitcast(FP8X4), scales=rank_scales[t][:], in_=rank_grouped[t][:])
+
+        def make_jump(i):
+            n, t = divmod(i, TILES)
+            jump[i] = keep.tile([P, GROUP], F32, name="jump%d" % (i % 4))
+            nc.scalar.activation(
+                out=jump[i][:], in_=tele_all[:, GROUP * n : GROUP * (n + 1)], func=ACT.Copy, scale=rest_col[:, t : t + 1]
+            )
+
+        def multiply(i):
+            n, t = divmod(i, TILES)
+            acc[i] = psum.tile([P, GROUP], F32, name="acc%d" % (i % 4))
+            for g in range(GROUPS):
+                if n == 0:
+                    scale = first_scales[:, g, :]
+                else:
+                    scale = later_scales[:, g, GROUP * (n - 1) : GROUP * n]
+                nc.tensor.matmul_mx(
+                    out=acc[i][:],
+                    lhsT=rank_codes[t][:, P * g : P * (g + 1)].bitcast(FP8X4),
+                    lhsT_scale=rank_scales[t][:, P * g : P * (g + 1)],
+                    rhs=link_words[n][:, g, :].bitcast(FP4X4),
+                    rhs_scale=scale,
+                    start=(g == 0),
+                    stop=(g == GROUPS - 1),
+                )
+
+        def finish(i):
+            n, t = divmod(i, TILES)
+            y[i] = keep.tile([P, GROUP], F32, name="y%d" % (i % 24))
+            nc.vector.scalar_tensor_tensor(
+                out=y[i][:], in0=acc[i][:], scalar=damp_col[:, t : t + 1], in1=jump[i][:], op0=ALU.mult, op1=ALU.add
+            )
+            nc.sync.dma_start(out=out_0[P * t : P * (t + 1), GROUP * n : GROUP * (n + 1)], in_=y[i][:])
+
+        def round_y(i, on_scalar=False):
+            y_bf[i] = keep.tile([P, GROUP], BF16, name="y_bf%d" % (i % 16))
+            dst = y_bf[i][:].rearrange("p (u w e) -> p u w e", u=2, e=2)
+            src = y[i][:].rearrange("p (w u e) -> p u w e", u=2, e=2)
+            if on_scalar:
+                nc.scalar.copy(out=dst, in_=src)
+            else:
+                nc.vector.tensor_copy(out=dst, in_=src)
+
+        def turn_units(units):
+            quad = units[0] // 4
+            if quad not in y_grouped:
+                y_grouped[quad] = keep.tile([P, 4 * GROUP], BF16, name="y_grouped%d" % (quad % 3), align_bytes=256)
+            bank = turn_bank()
+            for j, i in enumerate(units):
+                words = y_bf[i][:].bitcast(F32)
+                for u in range(2):
+                    nc.tensor.transpose(bank[:, 2 * j + u, :], words[:, P * u : P * (u + 1)], ident[:])
+            w0 = 256 * (units[0] % 4)
+            dst = y_grouped[quad][:].bitcast(F32)[:, w0 : w0 + 256 * len(units)]
+            nc.scalar.copy(
+                out=dst.rearrange("p (j r u) -> p j r u", r=P, u=2),
+                in_=bank[:, 0 : 2 * len(units), :].rearrange("p (j u) r -> p j r u", u=2),
+            )
+
+        def quantize_y(first, count):
+            n, t = divmod(first, TILES)
+            c0 = GROUP * (first % 4)
+            cols = slice(P * t, P * (t + count))
+            nc.vector.quantize_mx(
+                out=out_codes[n][:, cols].bitcast(FP8X4),
+                scales=out_scales[:, n, cols],
+                in_=y_grouped[first // 4][:, c0 : c0 + GROUP * count],
+            )
+
+        def store_codes(first, count):
+            n, t = divmod(first, TILES)
+            cols = slice(P * t, P * (t + count))
+            dst = out_1[n].rearrange("p m t -> p (m t)").bitcast(I32)
+            nc.sync.dma_start(out=dst[:, cols], in_=out_codes[n][:, cols].bitcast(I32))
+
+        def store_scales(n0, n1, queues):
+            for q in range(QUADRANTS):
+                dst = out_2[n0:n1, SCALE_ROWS * q : SCALE_ROWS * (q + 1), :].bitcast(I32).rearrange("g r m -> r g m")
+                queues[q % len(queues)].dma_start(
+                    out=dst, in_=out_scales[:].bitcast(I32)[32 * q : 32 * q + SCALE_ROWS, n0:n1, :]
+                )
+
+        for i in range(UNITS):
+            if i >= 1:
+                finish(i - 1)
+            if 2 <= i <= 30:
+                round_y(i - 2)
+            for t in RANK_TURNS.get(i, []):
+                turn_ranks(t)
+                if t == 0:
+                    make_jump(0)
+            for pair in PAIR_TURNS.get(i, []):
+                turn_units([2 * pair, 2 * pair + 1])
+            if i + 1 < UNITS:
+                make_jump(i + 1)
+            for t in RANK_TURNS.get(i, []):
+                quantize_ranks(t)
+            for quad in QUAD_QUANTS.get(i, []):
+                quantize_y(4 * quad, 4)
+                store_codes(4 * quad, 4)
+                if quad % 2 == 1:
+                    store_scales(quad // 2, quad // 2 + 1, [nc.sync])
+            if i == 30:
+                round_y(29, on_scalar=True)
+            multiply(i)
+
+        round_y(30, on_scalar=True)
+        finish(31)
+        turn_units([28, 29])
+        turn_units([30])
+        round_y(31)
+        quantize_y(28, 2)
+        turn_units([31])
+        quantize_y(30, 2)
+        store_codes(28, 4)
+        store_scales(GROUPS - 1, GROUPS, [nc.scalar, nc.sync])

@@ -24,9 +24,43 @@ UNITS = GROUPS * TILES
 QUADRANTS = 4
 SCALE_ROWS = 4
 
-RANK_TURNS = {0: [0, 1], 1: [2], 2: [3, 4], 4: [5, 6], 6: [7]}
-PAIR_TURNS = {6: [0, 1], 14: [2, 3, 4, 5], 22: [6, 7, 8, 9], 30: [10, 11, 12, 13]}
-QUAD_QUANTS = {7: [0], 14: [1], 15: [2], 22: [3], 23: [4], 30: [5, 6]}
+PROGRAM = """
+LR.0.0.1 LR.0.1.2 LR.1.0.1 LR.1.1.2 LS0 LL.0.0.2 LL.0.2.4 LR.2.0.2 LR.3.0.2 LR.4.0.2 LR.5.0.2 LR.6.0.2 LR.7.0.2 LS1 LL.1.0.4 LL.2.0.4 LL.3.0.4
+C S.0.0.1.v S.0.1.2.v R.0.0.a R.0.1.a S.1.0.1.v S.1.1.2.v QR.0.0.1 QR.0.1.2 R.1.0.a J.0 R.1.1.a J.1 J.2 J.3 S.2.0.2.v QR.1.0.2 M.0
+R.2.0.a R.2.1.a J.4 S.3.0.2.v F.0 M.1
+S.4.0.2.v QR.2.0.2 F.1 R.3.0.a R.3.1.a R.4.0.a R.4.1.a B.0.a J.5 QR.3.0.1 QR.3.1.2 M.2
+S.5.0.2.v QR.4.0.2 S.6.0.2.v B.1.a F.2 M.3
+R.5.0.a R.5.1.a R.6.0.a R.6.1.a F.3 B.2.a J.6 QR.5.0.1 QR.5.1.2 M.4
+S.7.0.2.v QR.6.0.2 B.3.v F.4 M.5
+R.7.0.a R.7.1.a J.7 Y.0.2.a Y.2.2.a F.5 QR.7.0.1 QR.7.1.2 B.4.v M.6
+J.8 F.6 B.5.v J.9 QY.0.4 SC.0.4 M.7
+F.7 B.6.v J.10 M.8
+ F.8 B.7.v J.11 M.9
+ F.9 B.8.v J.12 M.10
+ F.10 B.9.v J.13 M.11
+ F.11 B.10.v J.14 M.12
+ F.12 B.11.v J.15 M.13
+ F.13 B.12.v Y.4.2.a Y.6.2.a Y.8.2.a Y.10.2.a J.16 QY.4.4 SC.4.4 SS.0 M.14
+ F.14 B.13.v J.17 QY.8.4 SC.8.4 M.15
+ F.15 B.14.v J.18 M.16
+ F.16 B.15.v J.19 M.17
+ F.17 B.16.v J.20 M.18
+ F.18 B.17.v J.21 M.19
+ F.19 B.18.v J.22 M.20
+ F.20 B.19.v J.23 M.21
+ F.21 B.20.v Y.12.2.a Y.14.2.a Y.16.2.a Y.18.2.a J.24 QY.12.4 SC.12.4 SS.1 M.22
+ F.22 B.21.v J.25 QY.16.4 SC.16.4 M.23
+ F.23 B.22.v J.26 M.24
+ F.24 B.23.v J.27 M.25
+ F.25 B.24.v J.28 M.26
+ F.26 B.25.v J.29 M.27
+ F.27 B.26.v J.30 M.28
+ F.28 B.27.v J.31 M.29
+
+F.29 B.28.v Y.20.2.a Y.22.2.a Y.24.2.a Y.26.2.v QY.20.4 SC.20.4 SS.2 B.29.a M.30
+F.30 QY.24.4 SC.24.4 B.30.a M.31
+FR.31 F.31 Y.28.2.a Y.30.2.a QY.28.2 SC.28.2 QY.30.2 SC.30.2 SE.3
+"""
 
 
 def tile_signed_link_rank_step_g4_kernel(
@@ -63,15 +97,22 @@ def tile_signed_link_rank_step_g4_kernel(
 
         nc.scalar.dma_start(out=tele_words[:], in_=teleport.rearrange("(p c) -> p c", p=P).bitcast(F32))
         nc.scalar.dma_start(out=damp_rows[:], in_=damp.rearrange("(t p) -> t p", p=P))
-        nc.vector.memset(first_scales[:].rearrange("p g n -> p (g n)").bitcast(I32), 0)
         nc.vector.memset(warm[:], 0.0)
+        nc.vector.memset(first_scales[:].rearrange("p g n -> p (g n)").bitcast(I32), 0)
         nc.vector.memset(damp_wide[:], 0.0)
         nc.vector.memset(later_scales[:].rearrange("p g n -> p (g n)").bitcast(I32), 0)
         nc.scalar.activation(out=warm[:, 4:5], in_=warm[:, 0:1], func=ACT.Copy)
         make_identity(nc, ident[:])
 
-        def load_ranks(t, c0, c1):
-            nc.sync.dma_start(out=raw[t][:, c0:c1], in_=ranks[P * t : P * (t + 1), c0:c1])
+        def copy(engine, out, in_):
+            if engine == "a":
+                nc.scalar.copy(out=out, in_=in_)
+            else:
+                nc.vector.tensor_copy(out=out, in_=in_)
+
+        def load_ranks(t, h0, h1):
+            cols = slice(h0 * PAGES // 2, h1 * PAGES // 2)
+            nc.sync.dma_start(out=raw[t][:, cols], in_=ranks[P * t : P * (t + 1), cols])
 
         def load_scales(plane, c0, c1):
             rows = links_scales[:, :, c0:c1].bitcast(I32).rearrange("g (q r) n -> r q g n", r=SCALE_ROWS)
@@ -82,36 +123,21 @@ def tile_signed_link_rank_step_g4_kernel(
             src = links_words[g0:g1, :, 2 * GROUP * n : 2 * GROUP * (n + 1)].bitcast(I32)
             nc.sync.dma_start(out=link_words[n][:].bitcast(I32)[:, g0:g1, :], in_=src.rearrange("g p w -> p g w"))
 
-        load_ranks(0, 0, PAGES // 2)
-        load_ranks(0, PAGES // 2, PAGES)
-        load_ranks(1, 0, PAGES)
-        load_scales(first_scales, 0, GROUP)
-        load_links(0, 0, 2)
-        load_links(0, 2, 4)
-        for t in range(2, TILES):
-            load_ranks(t, 0, PAGES)
-        load_scales(later_scales, GROUP, PAGES)
-        for n in range(1, GROUPS):
-            load_links(n, 0, GROUPS)
-
-        tele_view = tele_all[:].bitcast(F32).rearrange("p (j h c) -> p h j c", h=2, c=4)
-        for h in range(2):
-            bank = turn_bank()
-            for c in range(4):
-                col = 4 * h + c
-                nc.tensor.transpose(bank[:, c, :], tele_words[:, col : col + 1].to_broadcast([P, P]), ident[:])
-            if h == 0:
+        def constants():
+            nc.vector.tensor_copy(out=damp_wide[0:TILES, :], in_=damp_rows[:])
+            tele_view = tele_all[:].bitcast(F32).rearrange("p (j h c) -> p h j c", h=2, c=4)
+            for h in range(2):
+                bank = turn_bank()
+                for c in range(4):
+                    col = 4 * h + c
+                    nc.tensor.transpose(bank[:, c, :], tele_words[:, col : col + 1].to_broadcast([P, P]), ident[:])
                 nc.scalar.copy(out=tele_view[:, h], in_=bank[:].rearrange("p c j -> p j c"))
-            else:
-                nc.vector.tensor_copy(out=tele_view[:, h], in_=bank[:].rearrange("p c j -> p j c"))
-        nc.vector.tensor_copy(out=damp_wide[0:TILES, :], in_=damp_rows[:])
-        bank = turn_bank()
-        nc.tensor.transpose(bank[:, 0, :], damp_wide[:], ident[:])
-        nc.vector.tensor_copy(out=damp_col[:], in_=bank[:, 0, 0:TILES])
-        nc.vector.tensor_scalar(
-            out=rest_col[:], in0=bank[:, 0, 0:TILES], scalar1=-1.0, scalar2=1.0, op0=ALU.mult, op1=ALU.add
-        )
+            bank = turn_bank()
+            nc.tensor.transpose(bank[:, 0, :], damp_wide[:], ident[:])
+            nc.scalar.copy(out=damp_col[:], in_=bank[:, 0, 0:TILES])
+            nc.scalar.activation(out=rest_col[:], in_=bank[:, 0, 0:TILES], func=ACT.Copy, scale=-1.0, bias=1.0)
 
+        rank_sorted = {}
         rank_grouped = {}
         y_grouped = {}
         acc = {}
@@ -119,28 +145,40 @@ def tile_signed_link_rank_step_g4_kernel(
         y = {}
         y_bf = {}
 
-        def turn_ranks(t):
-            grouped = keep.tile([P, PAGES], BF16, name="rank_grouped%d" % (t % 3), align_bytes=256)
-            rank_grouped[t] = grouped
-            words = raw[t][:].bitcast(F32)
-            for half in range(2):
-                bank = turn_bank()
-                for k in range(4):
-                    g, u = 2 * half + k // 2, k % 2
-                    nc.tensor.transpose(bank[:, k, :], words[:, 256 * g + u : 256 * (g + 1) : 2], ident[:])
-                dst = grouped[:].bitcast(F32)[:, 512 * half : 512 * (half + 1)].rearrange("p (g r u) -> p g r u", g=2, u=2)
-                src = bank[:].rearrange("p (g u) r -> p g r u", u=2)
-                if t == 0 and half == 1:
-                    nc.vector.tensor_copy(out=dst, in_=src)
-                else:
-                    nc.scalar.copy(out=dst, in_=src)
+        def sort_ranks(t, h0, h1, engine):
+            if t not in rank_sorted:
+                rank_sorted[t] = keep.tile([P, PAGES // 2], F32, name="rank_sorted%d" % (t % 3))
+            cols = slice(512 * h0, 512 * h1)
+            copy(
+                engine,
+                rank_sorted[t][:, cols].rearrange("p (g u w) -> p g u w", u=2, w=P),
+                raw[t][:].bitcast(F32)[:, cols].rearrange("p (g w u) -> p g u w", u=2, w=P),
+            )
 
-        def quantize_ranks(t):
-            nc.vector.quantize_mx(out=rank_codes[t][:].bitcast(FP8X4), scales=rank_scales[t][:], in_=rank_grouped[t][:])
+        def turn_ranks(t, half, engine):
+            if t not in rank_grouped:
+                rank_grouped[t] = keep.tile([P, PAGES], BF16, name="rank_grouped%d" % (t % 3), align_bytes=256)
+            bank = turn_bank()
+            for k in range(4):
+                g, u = 2 * half + k // 2, k % 2
+                if t in rank_sorted:
+                    words = rank_sorted[t][:, 256 * g + P * u : 256 * g + P * (u + 1)]
+                else:
+                    words = raw[t][:].bitcast(F32)[:, 256 * g + u : 256 * (g + 1) : 2]
+                nc.tensor.transpose(bank[:, k, :], words, ident[:])
+            dst = rank_grouped[t][:].bitcast(F32)[:, 512 * half : 512 * (half + 1)]
+            copy(engine, dst.rearrange("p (g r u) -> p g r u", g=2, u=2), bank[:].rearrange("p (g u) r -> p g r u", u=2))
+
+        def quantize_ranks(t, h0, h1):
+            nc.vector.quantize_mx(
+                out=rank_codes[t][:, 256 * h0 : 256 * h1].bitcast(FP8X4),
+                scales=rank_scales[t][:, 256 * h0 : 256 * h1],
+                in_=rank_grouped[t][:, 1024 * h0 : 1024 * h1],
+            )
 
         def make_jump(i):
             n, t = divmod(i, TILES)
-            jump[i] = keep.tile([P, GROUP], F32, name="jump%d" % (i % 4))
+            jump[i] = keep.tile([P, GROUP], F32, name="jump%d" % (i % 6))
             nc.scalar.activation(
                 out=jump[i][:], in_=tele_all[:, GROUP * n : GROUP * (n + 1)], func=ACT.Copy, scale=rest_col[:, t : t + 1]
             )
@@ -171,29 +209,42 @@ def tile_signed_link_rank_step_g4_kernel(
             )
             nc.sync.dma_start(out=out_0[P * t : P * (t + 1), GROUP * n : GROUP * (n + 1)], in_=y[i][:])
 
-        def round_y(i, on_scalar=False):
+        def round_y(i, engine):
             y_bf[i] = keep.tile([P, GROUP], BF16, name="y_bf%d" % (i % 16))
-            dst = y_bf[i][:].rearrange("p (u w e) -> p u w e", u=2, e=2)
-            src = y[i][:].rearrange("p (w u e) -> p u w e", u=2, e=2)
-            if on_scalar:
-                nc.scalar.copy(out=dst, in_=src)
-            else:
-                nc.vector.tensor_copy(out=dst, in_=src)
+            copy(
+                engine,
+                y_bf[i][:].rearrange("p (u w e) -> p u w e", u=2, e=2),
+                y[i][:].rearrange("p (w u e) -> p u w e", u=2, e=2),
+            )
 
-        def turn_units(units):
-            quad = units[0] // 4
+        def finish_rounded(i):
+            n, t = divmod(i, TILES)
+            y_bf[i] = keep.tile([P, GROUP], BF16, name="y_bf%d" % (i % 16))
+            for u in range(2):
+                nc.vector.scalar_tensor_tensor(
+                    out=y_bf[i][:].rearrange("p (u w e) -> p u w e", u=2, e=2)[:, u],
+                    in0=acc[i][:].rearrange("p (w u e) -> p u w e", u=2, e=2)[:, u],
+                    scalar=damp_col[:, t : t + 1],
+                    in1=jump[i][:].rearrange("p (w u e) -> p u w e", u=2, e=2)[:, u],
+                    op0=ALU.mult,
+                    op1=ALU.add,
+                )
+
+        def turn_units(first, count, engine):
+            quad = first // 4
             if quad not in y_grouped:
                 y_grouped[quad] = keep.tile([P, 4 * GROUP], BF16, name="y_grouped%d" % (quad % 3), align_bytes=256)
             bank = turn_bank()
-            for j, i in enumerate(units):
-                words = y_bf[i][:].bitcast(F32)
+            for j in range(count):
+                words = y_bf[first + j][:].bitcast(F32)
                 for u in range(2):
                     nc.tensor.transpose(bank[:, 2 * j + u, :], words[:, P * u : P * (u + 1)], ident[:])
-            w0 = 256 * (units[0] % 4)
-            dst = y_grouped[quad][:].bitcast(F32)[:, w0 : w0 + 256 * len(units)]
-            nc.scalar.copy(
-                out=dst.rearrange("p (j r u) -> p j r u", r=P, u=2),
-                in_=bank[:, 0 : 2 * len(units), :].rearrange("p (j u) r -> p j r u", u=2),
+            w0 = 256 * (first % 4)
+            dst = y_grouped[quad][:].bitcast(F32)[:, w0 : w0 + 256 * count]
+            copy(
+                engine,
+                dst.rearrange("p (j r u) -> p j r u", r=P, u=2),
+                bank[:, 0 : 2 * count, :].rearrange("p (j u) r -> p j r u", u=2),
             )
 
         def quantize_y(first, count):
@@ -212,44 +263,52 @@ def tile_signed_link_rank_step_g4_kernel(
             dst = out_1[n].rearrange("p m t -> p (m t)").bitcast(I32)
             nc.sync.dma_start(out=dst[:, cols], in_=out_codes[n][:, cols].bitcast(I32))
 
-        def store_scales(n0, n1, queues):
-            for q in range(QUADRANTS):
-                dst = out_2[n0:n1, SCALE_ROWS * q : SCALE_ROWS * (q + 1), :].bitcast(I32).rearrange("g r m -> r g m")
-                queues[q % len(queues)].dma_start(
-                    out=dst, in_=out_scales[:].bitcast(I32)[32 * q : 32 * q + SCALE_ROWS, n0:n1, :]
+        def store_scales(n, queues):
+            for j, q in enumerate((0, 2, 1, 3)):
+                dst = out_2[n, SCALE_ROWS * q : SCALE_ROWS * (q + 1), :].bitcast(I32)
+                queues[j % len(queues)].dma_start(
+                    out=dst, in_=out_scales[:].bitcast(I32)[32 * q : 32 * q + SCALE_ROWS, n, :]
                 )
 
-        for i in range(UNITS):
-            if i >= 1:
-                finish(i - 1)
-            if 2 <= i <= 30:
-                round_y(i - 2)
-            for t in RANK_TURNS.get(i, []):
-                turn_ranks(t)
-                if t == 0:
-                    make_jump(0)
-            for pair in PAIR_TURNS.get(i, []):
-                turn_units([2 * pair, 2 * pair + 1])
-            if i + 1 < UNITS:
-                make_jump(i + 1)
-            for t in RANK_TURNS.get(i, []):
-                quantize_ranks(t)
-            for quad in QUAD_QUANTS.get(i, []):
-                quantize_y(4 * quad, 4)
-                store_codes(4 * quad, 4)
-                if quad % 2 == 1:
-                    store_scales(quad // 2, quad // 2 + 1, [nc.sync])
-            if i == 30:
-                round_y(29, on_scalar=True)
-            multiply(i)
-
-        round_y(30, on_scalar=True)
-        finish(31)
-        turn_units([28, 29])
-        turn_units([30])
-        round_y(31)
-        quantize_y(28, 2)
-        turn_units([31])
-        quantize_y(30, 2)
-        store_codes(28, 4)
-        store_scales(GROUPS - 1, GROUPS, [nc.scalar, nc.sync])
+        for token in PROGRAM.split():
+            parts = token.split(".")
+            kind = parts[0]
+            a = [int(x) if x not in ("a", "v") else x for x in parts[1:]]
+            if kind == "LR":
+                load_ranks(*a)
+            elif kind == "LS0":
+                load_scales(first_scales, 0, GROUP)
+            elif kind == "LS1":
+                load_scales(later_scales, GROUP, PAGES)
+            elif kind == "LL":
+                load_links(*a)
+            elif kind == "C":
+                constants()
+            elif kind == "S":
+                sort_ranks(*a)
+            elif kind == "R":
+                turn_ranks(*a)
+            elif kind == "QR":
+                quantize_ranks(*a)
+            elif kind == "J":
+                make_jump(*a)
+            elif kind == "M":
+                multiply(*a)
+            elif kind == "F":
+                finish(*a)
+            elif kind == "FR":
+                finish_rounded(*a)
+            elif kind == "B":
+                round_y(*a)
+            elif kind == "Y":
+                turn_units(*a)
+            elif kind == "QY":
+                quantize_y(*a)
+            elif kind == "SC":
+                store_codes(*a)
+            elif kind == "SS":
+                store_scales(a[0], [nc.sync])
+            elif kind == "SE":
+                store_scales(a[0], [nc.scalar, nc.sync])
+            else:
+                raise ValueError(kind)

from contextlib import ExitStack

import concourse.mybir as mybir
from concourse.masks import make_identity

SURFERS, PAGES = 1024, 2048
FLOPS = 2 * SURFERS * PAGES * PAGES

F32 = mybir.dt.float32
BF16 = mybir.dt.bfloat16
I32 = mybir.dt.int32
U32 = mybir.dt.uint32
U8 = mybir.dt.uint8
FP8X4 = mybir.dt.float8_e4m3fn_x4
FP4X4 = mybir.dt.float4_e2m1fn_x4
ALU = mybir.AluOpType
ACT = mybir.ActivationFunctionType

P = 128
GROUP = 512
GROUPS = PAGES // GROUP
TILES = SURFERS // P
UNITS = GROUPS * TILES
QUADRANTS = 4
SCALE_ROWS = 4

PROGRAM = """
LR.0.0.1 LR.0.1.2 LR.1.0.1 LR.1.1.2 LS0 LL.0.0.2 LL.0.2.4 LR.2.0.2 LR.3.0.2 LR.4.0.2 LR.5.0.2 LR.6.0.2 LR.7.0.2 LS1 LL.1.0.4 LL.2.0.4 LL.3.0.4
C S.0.0.1.v S.0.1.2.v R.0.0.a R.0.1.a S.1.0.1.v S.1.1.2.v QR.0.0.1 QR.0.1.2 R.1.0.a J.0 R.1.1.a J.1 J.2 J.3 S.2.0.2.v QR.1.0.2 M.0
R.2.0.a R.2.1.a J.4 S.3.0.2.v F.0 M.1
S.4.0.2.v QR.2.0.2 F.1 R.3.0.a R.3.1.a R.4.0.a R.4.1.a B.0.a J.5 QR.3.0.1 QR.3.1.2 M.2
S.5.0.2.v QR.4.0.2 S.6.0.2.v B.1.a F.2 M.3
R.5.0.a R.5.1.a R.6.0.a R.6.1.a F.3 B.2.a J.6 QR.5.0.1 QR.5.1.2 M.4
S.7.0.2.v QR.6.0.2 B.3.v F.4 M.5
R.7.0.a R.7.1.a J.7 Y.0.2.a Y.2.2.a F.5 QR.7.0.1 QR.7.1.2 B.4.v M.6
J.8 F.6 B.5.v J.9 QY.0.4 SC.0.4 M.7
F.7 B.6.v J.10 M.8
 F.8 B.7.v J.11 M.9
 F.9 B.8.v J.12 M.10
 F.10 B.9.v J.13 M.11
 F.11 B.10.v J.14 M.12
 F.12 B.11.v J.15 M.13
 F.13 B.12.v Y.4.2.a Y.6.2.a Y.8.2.a Y.10.2.a J.16 QY.4.4 SC.4.4 SS.0 M.14
 F.14 B.13.v J.17 QY.8.4 SC.8.4 M.15
 F.15 B.14.v J.18 M.16
 F.16 B.15.v J.19 M.17
 F.17 B.16.v J.20 M.18
 F.18 B.17.v J.21 M.19
 F.19 B.18.v J.22 M.20
 F.20 B.19.v J.23 M.21
 F.21 B.20.v Y.12.2.a Y.14.2.a Y.16.2.a Y.18.2.a J.24 QY.12.4 SC.12.4 SS.1 M.22
 F.22 B.21.v J.25 QY.16.4 SC.16.4 M.23
 F.23 B.22.v J.26 M.24
 F.24 B.23.v J.27 M.25
 F.25 B.24.v J.28 M.26
 F.26 B.25.v J.29 M.27
 F.27 B.26.v J.30 M.28
 F.28 B.27.v J.31 M.29

F.29 B.28.v Y.20.2.a Y.22.2.a Y.24.2.a Y.26.2.v QY.20.4 SC.20.4 SS.2 B.29.a M.30
F.30 QY.24.4 SC.24.4 B.30.a M.31
FR.31 F.31 Y.28.2.a Y.30.2.a QY.28.2 SC.28.2 QY.30.2 SC.30.2 SE.3
"""


def tile_signed_link_rank_step_g4_kernel(
    tc, ranks, links_words, links_scales, damp, teleport, out_0, out_1, out_2
):
    nc = tc.nc
    with ExitStack() as ctx:
        keep = ctx.enter_context(tc.tile_pool(name="keep", bufs=1))
        psum = ctx.enter_context(tc.psum_pool(name="psum", bufs=1))
        ctx.enter_context(tc.manual_schedule())

        turn_count = []

        def turn_bank():
            turn_count.append(0)
            return psum.tile([P, 4, P], F32, name="turn%d" % (len(turn_count) % 4))

        ident = keep.tile([P, P], F32, name="ident")
        tele_words = keep.tile([P, 8], F32, name="tele_words")
        damp_rows = keep.tile([TILES, P], BF16, name="damp_rows")
        damp_wide = keep.tile([P, P], F32, name="damp_wide")
        damp_col = keep.tile([P, TILES], F32, name="damp_col")
        rest_col = keep.tile([P, TILES], F32, name="rest_col")
        tele_all = keep.tile([P, PAGES], BF16, name="tele_all")
        warm = keep.tile([P, 8], F32, name="warm")
        raw = [keep.tile([P, PAGES], BF16, name="raw%d" % t) for t in range(TILES)]
        rank_codes = [keep.tile([P, GROUP], U32, name="rank_codes%d" % t, align_bytes=256) for t in range(TILES)]
        rank_scales = [keep.tile([P, GROUP], U8, name="rank_scales%d" % t, align_bytes=256) for t in range(TILES)]
        link_words = [keep.tile([P, GROUPS, 2 * GROUP], U8, name="link_words%d" % n, align_bytes=256) for n in range(GROUPS)]
        first_scales = keep.tile([P, GROUPS, GROUP], U8, name="first_scales", align_bytes=256)
        later_scales = keep.tile([P, GROUPS, PAGES - GROUP], U8, name="later_scales", align_bytes=256)
        out_codes = [keep.tile([P, SURFERS], U32, name="out_codes%d" % n, align_bytes=256) for n in range(GROUPS)]
        out_scales = keep.tile([P, GROUPS, SURFERS], U8, name="out_scales", align_bytes=256)

        nc.scalar.dma_start(out=tele_words[:], in_=teleport.rearrange("(p c) -> p c", p=P).bitcast(F32))
        nc.scalar.dma_start(out=damp_rows[:], in_=damp.rearrange("(t p) -> t p", p=P))
        nc.vector.memset(warm[:], 0.0)
        nc.vector.memset(first_scales[:].rearrange("p g n -> p (g n)").bitcast(I32), 0)
        nc.vector.memset(damp_wide[:], 0.0)
        nc.vector.memset(later_scales[:].rearrange("p g n -> p (g n)").bitcast(I32), 0)
        nc.scalar.activation(out=warm[:, 4:5], in_=warm[:, 0:1], func=ACT.Copy)
        make_identity(nc, ident[:])

        def copy(engine, out, in_):
            if engine == "a":
                nc.scalar.copy(out=out, in_=in_)
            else:
                nc.vector.tensor_copy(out=out, in_=in_)

        def load_ranks(t, h0, h1):
            cols = slice(h0 * PAGES // 2, h1 * PAGES // 2)
            nc.sync.dma_start(out=raw[t][:, cols], in_=ranks[P * t : P * (t + 1), cols])

        def load_scales(plane, c0, c1):
            rows = links_scales[:, :, c0:c1].bitcast(I32).rearrange("g (q r) n -> r q g n", r=SCALE_ROWS)
            for r in range(SCALE_ROWS):
                nc.sync.dma_start(out=plane[:].bitcast(I32)[r:P:32, :, :], in_=rows[r])

        def load_links(n, g0, g1):
            src = links_words[g0:g1, :, 2 * GROUP * n : 2 * GROUP * (n + 1)].bitcast(I32)
            nc.sync.dma_start(out=link_words[n][:].bitcast(I32)[:, g0:g1, :], in_=src.rearrange("g p w -> p g w"))

        def constants():
            nc.vector.tensor_copy(out=damp_wide[0:TILES, :], in_=damp_rows[:])
            tele_view = tele_all[:].bitcast(F32).rearrange("p (j h c) -> p h j c", h=2, c=4)
            for h in range(2):
                bank = turn_bank()
                for c in range(4):
                    col = 4 * h + c
                    nc.tensor.transpose(bank[:, c, :], tele_words[:, col : col + 1].to_broadcast([P, P]), ident[:])
                nc.scalar.copy(out=tele_view[:, h], in_=bank[:].rearrange("p c j -> p j c"))
            bank = turn_bank()
            nc.tensor.transpose(bank[:, 0, :], damp_wide[:], ident[:])
            nc.scalar.copy(out=damp_col[:], in_=bank[:, 0, 0:TILES])
            nc.scalar.activation(out=rest_col[:], in_=bank[:, 0, 0:TILES], func=ACT.Copy, scale=-1.0, bias=1.0)

        rank_sorted = {}
        rank_grouped = {}
        y_grouped = {}
        acc = {}
        jump = {}
        y = {}
        y_bf = {}

        def sort_ranks(t, h0, h1, engine):
            if t not in rank_sorted:
                rank_sorted[t] = keep.tile([P, PAGES // 2], F32, name="rank_sorted%d" % (t % 3))
            cols = slice(512 * h0, 512 * h1)
            copy(
                engine,
                rank_sorted[t][:, cols].rearrange("p (g u w) -> p g u w", u=2, w=P),
                raw[t][:].bitcast(F32)[:, cols].rearrange("p (g w u) -> p g u w", u=2, w=P),
            )

        def turn_ranks(t, half, engine):
            if t not in rank_grouped:
                rank_grouped[t] = keep.tile([P, PAGES], BF16, name="rank_grouped%d" % (t % 3), align_bytes=256)
            bank = turn_bank()
            for k in range(4):
                g, u = 2 * half + k // 2, k % 2
                if t in rank_sorted:
                    words = rank_sorted[t][:, 256 * g + P * u : 256 * g + P * (u + 1)]
                else:
                    words = raw[t][:].bitcast(F32)[:, 256 * g + u : 256 * (g + 1) : 2]
                nc.tensor.transpose(bank[:, k, :], words, ident[:])
            dst = rank_grouped[t][:].bitcast(F32)[:, 512 * half : 512 * (half + 1)]
            copy(engine, dst.rearrange("p (g r u) -> p g r u", g=2, u=2), bank[:].rearrange("p (g u) r -> p g r u", u=2))

        def quantize_ranks(t, h0, h1):
            nc.vector.quantize_mx(
                out=rank_codes[t][:, 256 * h0 : 256 * h1].bitcast(FP8X4),
                scales=rank_scales[t][:, 256 * h0 : 256 * h1],
                in_=rank_grouped[t][:, 1024 * h0 : 1024 * h1],
            )

        def make_jump(i):
            n, t = divmod(i, TILES)
            jump[i] = keep.tile([P, GROUP], F32, name="jump%d" % (i % 6))
            nc.scalar.activation(
                out=jump[i][:], in_=tele_all[:, GROUP * n : GROUP * (n + 1)], func=ACT.Copy, scale=rest_col[:, t : t + 1]
            )

        def multiply(i):
            n, t = divmod(i, TILES)
            acc[i] = psum.tile([P, GROUP], F32, name="acc%d" % (i % 4))
            for g in range(GROUPS):
                if n == 0:
                    scale = first_scales[:, g, :]
                else:
                    scale = later_scales[:, g, GROUP * (n - 1) : GROUP * n]
                nc.tensor.matmul_mx(
                    out=acc[i][:],
                    lhsT=rank_codes[t][:, P * g : P * (g + 1)].bitcast(FP8X4),
                    lhsT_scale=rank_scales[t][:, P * g : P * (g + 1)],
                    rhs=link_words[n][:, g, :].bitcast(FP4X4),
                    rhs_scale=scale,
                    start=(g == 0),
                    stop=(g == GROUPS - 1),
                )

        def finish(i):
            n, t = divmod(i, TILES)
            y[i] = keep.tile([P, GROUP], F32, name="y%d" % (i % 24))
            nc.vector.scalar_tensor_tensor(
                out=y[i][:], in0=acc[i][:], scalar=damp_col[:, t : t + 1], in1=jump[i][:], op0=ALU.mult, op1=ALU.add
            )
            nc.sync.dma_start(out=out_0[P * t : P * (t + 1), GROUP * n : GROUP * (n + 1)], in_=y[i][:])

        def round_y(i, engine):
            y_bf[i] = keep.tile([P, GROUP], BF16, name="y_bf%d" % (i % 16))
            copy(
                engine,
                y_bf[i][:].rearrange("p (u w e) -> p u w e", u=2, e=2),
                y[i][:].rearrange("p (w u e) -> p u w e", u=2, e=2),
            )

        def finish_rounded(i):
            n, t = divmod(i, TILES)
            y_bf[i] = keep.tile([P, GROUP], BF16, name="y_bf%d" % (i % 16))
            for u in range(2):
                nc.vector.scalar_tensor_tensor(
                    out=y_bf[i][:].rearrange("p (u w e) -> p u w e", u=2, e=2)[:, u],
                    in0=acc[i][:].rearrange("p (w u e) -> p u w e", u=2, e=2)[:, u],
                    scalar=damp_col[:, t : t + 1],
                    in1=jump[i][:].rearrange("p (w u e) -> p u w e", u=2, e=2)[:, u],
                    op0=ALU.mult,
                    op1=ALU.add,
                )

        def turn_units(first, count, engine):
            quad = first // 4
            if quad not in y_grouped:
                y_grouped[quad] = keep.tile([P, 4 * GROUP], BF16, name="y_grouped%d" % (quad % 3), align_bytes=256)
            bank = turn_bank()
            for j in range(count):
                words = y_bf[first + j][:].bitcast(F32)
                for u in range(2):
                    nc.tensor.transpose(bank[:, 2 * j + u, :], words[:, P * u : P * (u + 1)], ident[:])
            w0 = 256 * (first % 4)
            dst = y_grouped[quad][:].bitcast(F32)[:, w0 : w0 + 256 * count]
            copy(
                engine,
                dst.rearrange("p (j r u) -> p j r u", r=P, u=2),
                bank[:, 0 : 2 * count, :].rearrange("p (j u) r -> p j r u", u=2),
            )

        def quantize_y(first, count):
            n, t = divmod(first, TILES)
            c0 = GROUP * (first % 4)
            cols = slice(P * t, P * (t + count))
            nc.vector.quantize_mx(
                out=out_codes[n][:, cols].bitcast(FP8X4),
                scales=out_scales[:, n, cols],
                in_=y_grouped[first // 4][:, c0 : c0 + GROUP * count],
            )

        def store_codes(first, count):
            n, t = divmod(first, TILES)
            cols = slice(P * t, P * (t + count))
            dst = out_1[n].rearrange("p m t -> p (m t)").bitcast(I32)
            nc.sync.dma_start(out=dst[:, cols], in_=out_codes[n][:, cols].bitcast(I32))

        def store_scales(n, queues):
            for j, q in enumerate((0, 2, 1, 3)):
                dst = out_2[n, SCALE_ROWS * q : SCALE_ROWS * (q + 1), :].bitcast(I32)
                queues[j % len(queues)].dma_start(
                    out=dst, in_=out_scales[:].bitcast(I32)[32 * q : 32 * q + SCALE_ROWS, n, :]
                )

        for token in PROGRAM.split():
            parts = token.split(".")
            kind = parts[0]
            a = [int(x) if x not in ("a", "v") else x for x in parts[1:]]
            if kind == "LR":
                load_ranks(*a)
            elif kind == "LS0":
                load_scales(first_scales, 0, GROUP)
            elif kind == "LS1":
                load_scales(later_scales, GROUP, PAGES)
            elif kind == "LL":
                load_links(*a)
            elif kind == "C":
                constants()
            elif kind == "S":
                sort_ranks(*a)
            elif kind == "R":
                turn_ranks(*a)
            elif kind == "QR":
                quantize_ranks(*a)
            elif kind == "J":
                make_jump(*a)
            elif kind == "M":
                multiply(*a)
            elif kind == "F":
                finish(*a)
            elif kind == "FR":
                finish_rounded(*a)
            elif kind == "B":
                round_y(*a)
            elif kind == "Y":
                turn_units(*a)
            elif kind == "QY":
                quantize_y(*a)
            elif kind == "SC":
                store_codes(*a)
            elif kind == "SS":
                store_scales(a[0], [nc.sync])
            elif kind == "SE":
                store_scales(a[0], [nc.scalar, nc.sync])
            else:
                raise ValueError(kind)
